import numpy as np
import ml_dtypes


def mxq(x, axis, fmt="e4m3"):
    dtype, down = {"e4m3": (ml_dtypes.float8_e4m3fn, 7), "e5m2": (ml_dtypes.float8_e5m2, 14)}[fmt]
    v = np.moveaxis(np.asarray(x, np.float32).astype(ml_dtypes.bfloat16).astype(np.float64), axis, -1)
    blocks = v.reshape(v.shape[:-1] + (-1, 32))
    amax = np.abs(blocks).max(-1, keepdims=True)
    byte = np.maximum(np.where(amax > 0, np.frexp(amax)[1] - 1 + 127, 0) - down, 1)
    scale = np.exp2(byte - 127.0)
    codes = (blocks / scale).astype(np.float32).astype(dtype).astype(np.float64)
    return np.moveaxis((codes * scale).reshape(v.shape), -1, axis)


WIDE = False


def mx_kscale(k):
    if not WIDE:
        return np.ones(k)
    levels = np.array([10, -10, 5, -5, 0])
    if k % 512:
        return np.exp2(np.random.permutation(np.resize(levels, k // 32))).repeat(32)
    a = np.empty((k // 512, 16))
    for p in range(k // 512):
        a[p, :8] = np.random.permutation(np.resize(levels, 8))
        for g in range(8):
            far = levels[np.abs(levels - a[p, g]) >= 10]
            a[p, g + 8] = far[np.random.randint(len(far))]
    return np.exp2(a.ravel()).repeat(32)


def f64(x):
    return np.asarray(x).astype(np.float64)


def striped(idx):
    return np.tile(np.asarray(idx).reshape(-1, 16).T, (8, 1)).astype(np.uint16)


def unstriped(offs):
    return offs[:16].T.reshape(-1).astype(np.int64)


E2M1 = np.array([0.0, 0.5, 1.0, 1.5, 2.0, 3.0, 4.0, 6.0, -0.0, -0.5, -1.0, -1.5, -2.0, -3.0, -4.0, -6.0])


def pack_weight(w, fmt):
    k, n = w.shape
    w = f64(np.asarray(w, np.float32).astype(ml_dtypes.bfloat16)).reshape(k // 32, 32, n)
    amax = np.abs(w).max(1)
    if fmt == "e4m3":
        byte = np.frexp(amax)[1] - 1 + 127 - 7
    else:
        mant, ex = np.frexp(amax / 6.0)
        byte = np.where(mant > 0.5, ex, ex - 1) + 127
    byte = np.clip(np.where(amax > 0, byte, 1), 1, 254)
    scaled = (w * np.exp2(127.0 - byte)[:, None, :]).reshape(k, n).astype(np.float32)
    by_word = np.ascontiguousarray(scaled.reshape(k // 512, 128, 4, n).transpose(0, 1, 3, 2))
    if fmt == "e4m3":
        words = by_word.astype(ml_dtypes.float8_e4m3fn).view(np.uint8)
    else:
        c = by_word.astype(ml_dtypes.float4_e2m1fn).view(np.uint8) & 0xF
        words = (c[..., 0::2] | (c[..., 1::2] << 4)).reshape(k // 512, 128, 2 * n)
    return np.ascontiguousarray(words), np.ascontiguousarray(byte.astype(np.uint8).reshape(k // 512, 16, n))


def unpack_weight(words, scales, fmt):
    g, _, n = scales.shape
    words = np.ascontiguousarray(words).reshape(g, 128, n, -1)
    if fmt == "e4m3":
        vals = words.view(ml_dtypes.float8_e4m3fn).astype(np.float64)
    else:
        nib = np.empty((g, 128, n, 4), np.uint8)
        nib[..., 0::2] = words & 0xF
        nib[..., 1::2] = words >> 4
        vals = E2M1[nib]
    vals = vals * np.repeat(np.exp2(scales.astype(np.float64) - 127.0), 8, axis=1)[..., None]
    return vals.transpose(0, 1, 3, 2).reshape(g * 512, n)


B, N, T, D, NQ = 1, 512, 2048, 512, 256


def setup_inputs():
    n = np.random.standard_normal
    idx = np.random.permutation(T)[:B * N]
    s = mx_kscale(D)[:, None]
    kp = pack_weight(n((D, T)) / s, "e4m3")
    cp = pack_weight(n((D, T)) / s / 12, "e4m3")
    return {
        "qT": (n((B, D, NQ)) * s * (8.00 / np.sqrt(D))).astype(np.float32),
        "k_words": kp[0],
        "k_scales": kp[1],
        "c_words": cp[0],
        "c_scales": cp[1],
        "offs": striped(idx),
    }


def reference(qT, k_words, k_scales, c_words, c_scales, offs):
    idx = unstriped(offs)
    pick = lambda x, which: x[:, which].reshape(x.shape[0], B, -1).transpose(1, 0, 2)
    k = unpack_weight(k_words, k_scales, "e4m3")
    kg = pick(k, idx)
    c = unpack_weight(c_words, c_scales, "e4m3")
    cg = pick(c, idx)
    qq = mxq(f64(qT), 1, "e4m3")
    a = (qq.transpose(0, 2, 1) @ kg) + (qq.transpose(0, 2, 1) @ cg)
    y = 20.0 * np.tanh(a / 20.0)
    return y

@@ -1,0 +1,113 @@
+from contextlib import ExitStack
+
+import concourse.mybir as mybir
+
+F32 = mybir.dt.float32
+BF16 = mybir.dt.bfloat16
+I32 = mybir.dt.int32
+U32 = mybir.dt.uint32
+U16 = mybir.dt.uint16
+U8 = mybir.dt.uint8
+FP8X4 = mybir.dt.float8_e4m3fn_x4
+TANH = mybir.ActivationFunctionType.Tanh
+
+P = 128
+PACK = 4
+D, NQ, T, N = 512, 256, 2048, 512
+CAP = 20.0
+HALF = N // 2
+C_ROW = 4
+
+FLOPS = 2 * 2 * D * NQ * N
+
+
+def tile_attend_residcap_topk_kernel(tc, qT, k_words, k_scales, c_words, c_scales, offs, out):
+    nc = tc.nc
+    with ExitStack() as ctx:
+        keep = ctx.enter_context(tc.tile_pool(name="keep", bufs=1))
+        psum = ctx.enter_context(tc.psum_pool(name="psum", bufs=1))
+
+        offsets = keep.tile([P, N // 16], U16, name="offsets")
+        q_raw = keep.tile([P, PACK, NQ], F32, name="q_raw", align_bytes=64)
+        kw_pool = keep.tile([P, T], I32, name="kw_pool", align_bytes=64)
+        cw_pool = keep.tile([P, T], I32, name="cw_pool", align_bytes=64)
+        ks_pool = keep.tile([P, T // 4], I32, name="ks_pool", align_bytes=64)
+        cs_pool = keep.tile([P, T // 4], I32, name="cs_pool", align_bytes=64)
+        zero = keep.tile([P, 1], F32, name="zero")
+        no_bias = keep.tile([P, 1], F32, name="no_bias")
+
+        nc.vector.memset(ks_pool[:], 0)
+        nc.vector.memset(cs_pool[:], 0)
+        nc.gpsimd.memset(zero[:], 0.0)
+        nc.scalar.activation(no_bias[:], zero[:], TANH)
+
+        def load_scales(eng, pool_tile, scales, first_row):
+            rows = scales[0].bitcast(I32)
+            for r in range(4):
+                eng.dma_start(pool_tile[first_row + r : P : 32, :], rows[r:16:4, :])
+
+        def load_words(pool_tile, words):
+            nc.sync.dma_start(pool_tile[:], words[0].rearrange("p n t -> p (n t)").bitcast(I32))
+
+        nc.sync.dma_start(offsets[:], offs)
+        nc.sync.dma_start(q_raw[:], qT[0].rearrange("(p j) w -> p j w", j=PACK))
+        load_scales(nc.sync, ks_pool, k_scales, 0)
+        load_words(kw_pool, k_words)
+        load_scales(nc.sync, cs_pool, c_scales, C_ROW)
+        load_words(cw_pool, c_words)
+
+        q_grouped = keep.tile([P, NQ, PACK], BF16, name="q_grouped", align_bytes=64)
+        q_codes = keep.tile([P, NQ], U32, name="q_codes", align_bytes=64)
+        q_scales = keep.tile([P, NQ], U8, name="q_scales", align_bytes=64)
+        kw = keep.tile([P, N], U32, name="kw", align_bytes=64)
+        cw = keep.tile([P, N], U32, name="cw", align_bytes=64)
+        ks = keep.tile([P, N], U8, name="ks", align_bytes=64)
+        cs = keep.tile([P, N], U8, name="cs", align_bytes=64)
+
+        q_by_column = q_raw[:].rearrange("p j w -> p w j")
+        nc.scalar.copy(q_grouped[:, 0:P, :], q_by_column[:, 0:P, :])
+        nc.vector.tensor_copy(q_grouped[:, P:NQ, :], q_by_column[:, P:NQ, :])
+        nc.vector.tensor_copy(ks[:], ks_pool[:].bitcast(U8).indirect(offsets[:]))
+        nc.vector.quantize_mx(
+            out=q_codes[:].bitcast(FP8X4),
+            scales=q_scales[:],
+            in_=q_grouped[:].rearrange("p w j -> p (w j)"),
+        )
+        nc.vector.tensor_copy(kw[:], kw_pool[:].bitcast(U32).indirect(offsets[:]))
+        nc.vector.tensor_copy(cs[:], cs_pool[:].bitcast(U8).indirect(offsets[:]))
+
+        acc = {}
+        for h in range(2):
+            for m in range(2):
+                acc[h, m] = psum.tile([P, HALF], F32, name="acc%d%d" % (h, m))
+
+        def product(h, m, words, scales, first_row, start):
+            slots = slice(h * HALF, (h + 1) * HALF)
+            rows = slice(m * P, (m + 1) * P)
+            nc.tensor.matmul_mx(
+                out=acc[h, m][:],
+                lhsT=q_codes[:, rows].bitcast(FP8X4),
+                lhsT_scale=q_scales[:, rows],
+                rhs=words[:, slots].bitcast(FP8X4),
+                rhs_scale=scales[first_row:P, slots],
+                start=start,
+                stop=not start,
+            )
+
+        for h in range(2):
+            for m in range(2):
+                product(h, m, kw, ks, 0, True)
+
+        for h in range(2):
+            slots = slice(h * HALF, (h + 1) * HALF)
+            cols = slice(h * HALF // 16, (h + 1) * HALF // 16)
+            nc.vector.tensor_copy(cw[:, slots], cw_pool[:].bitcast(U32).indirect(offsets[:, cols]))
+        for h in range(2):
+            slots = slice(h * HALF, (h + 1) * HALF)
+            for m in range(2):
+                product(h, m, cw, cs, C_ROW, False)
+                capped = keep.tile([P, HALF], F32, name="capped%d%d" % (h, m), align_bytes=64)
+                result = keep.tile([P, HALF], F32, name="result%d%d" % (h, m), align_bytes=64)
+                nc.scalar.activation(capped[:], acc[h, m][:], TANH, bias=no_bias[:], scale=1.0 / CAP)
+                nc.vector.tensor_scalar_mul(result[:], capped[:], CAP)
+                nc.sync.dma_start(out[0, m * P : (m + 1) * P, slots], result[:])

@@ -37,23 +37,23 @@ def tile_attend_residcap_topk_kernel(tc, qT, k_words, k_scales, c_words, c_scale
         no_bias = keep.tile([P, 1], F32, name="no_bias")
 
         nc.vector.memset(ks_pool[:], 0)
+        nc.vector.memset(zero[:], 0.0)
         nc.vector.memset(cs_pool[:], 0)
-        nc.gpsimd.memset(zero[:], 0.0)
-        nc.scalar.activation(no_bias[:], zero[:], TANH)
 
-        def load_scales(eng, pool_tile, scales, first_row):
+        def load_scales(engines, pool_tile, scales, first_row):
             rows = scales[0].bitcast(I32)
-            for r in range(4):
+            for r, eng in enumerate(engines):
                 eng.dma_start(pool_tile[first_row + r : P : 32, :], rows[r:16:4, :])
 
         def load_words(pool_tile, words):
             nc.sync.dma_start(pool_tile[:], words[0].rearrange("p n t -> p (n t)").bitcast(I32))
 
-        nc.sync.dma_start(offsets[:], offs)
         nc.sync.dma_start(q_raw[:], qT[0].rearrange("(p j) w -> p j w", j=PACK))
-        load_scales(nc.sync, ks_pool, k_scales, 0)
+        nc.sync.dma_start(offsets[:], offs)
+        load_scales([nc.sync, nc.sync, nc.scalar, nc.scalar], ks_pool, k_scales, 0)
+        nc.scalar.activation(no_bias[:], zero[:], TANH)
         load_words(kw_pool, k_words)
-        load_scales(nc.sync, cs_pool, c_scales, C_ROW)
+        load_scales([nc.sync] * 4, cs_pool, c_scales, C_ROW)
         load_words(cw_pool, c_words)
 
         q_grouped = keep.tile([P, NQ, PACK], BF16, name="q_grouped", align_bytes=64)
@@ -76,16 +76,15 @@ def tile_attend_residcap_topk_kernel(tc, qT, k_words, k_scales, c_words, c_scale
         nc.vector.tensor_copy(kw[:], kw_pool[:].bitcast(U32).indirect(offsets[:]))
         nc.vector.tensor_copy(cs[:], cs_pool[:].bitcast(U8).indirect(offsets[:]))
 
-        acc = {}
-        for h in range(2):
-            for m in range(2):
-                acc[h, m] = psum.tile([P, HALF], F32, name="acc%d%d" % (h, m))
+        units = [(0, 0, 256), (1, 0, 256), (0, 256, 256), (1, 256, 256)]
+        acc = [psum.tile([P, w], F32, name="acc%d" % u) for u, (m, s0, w) in enumerate(units)]
 
-        def product(h, m, words, scales, first_row, start):
-            slots = slice(h * HALF, (h + 1) * HALF)
+        def product(u, words, scales, first_row, start):
+            m, s0, w = units[u]
+            slots = slice(s0, s0 + w)
             rows = slice(m * P, (m + 1) * P)
             nc.tensor.matmul_mx(
-                out=acc[h, m][:],
+                out=acc[u][:],
                 lhsT=q_codes[:, rows].bitcast(FP8X4),
                 lhsT_scale=q_scales[:, rows],
                 rhs=words[:, slots].bitcast(FP8X4),
@@ -94,20 +93,21 @@ def tile_attend_residcap_topk_kernel(tc, qT, k_words, k_scales, c_words, c_scale
                 stop=not start,
             )
 
-        for h in range(2):
-            for m in range(2):
-                product(h, m, kw, ks, 0, True)
+        for u in range(len(units)):
+            product(u, kw, ks, 0, True)
 
         for h in range(2):
             slots = slice(h * HALF, (h + 1) * HALF)
             cols = slice(h * HALF // 16, (h + 1) * HALF // 16)
             nc.vector.tensor_copy(cw[:, slots], cw_pool[:].bitcast(U32).indirect(offsets[:, cols]))
-        for h in range(2):
-            slots = slice(h * HALF, (h + 1) * HALF)
-            for m in range(2):
-                product(h, m, cw, cs, C_ROW, False)
-                capped = keep.tile([P, HALF], F32, name="capped%d%d" % (h, m), align_bytes=64)
-                result = keep.tile([P, HALF], F32, name="result%d%d" % (h, m), align_bytes=64)
-                nc.scalar.activation(capped[:], acc[h, m][:], TANH, bias=no_bias[:], scale=1.0 / CAP)
-                nc.vector.tensor_scalar_mul(result[:], capped[:], CAP)
-                nc.sync.dma_start(out[0, m * P : (m + 1) * P, slots], result[:])
+        capped = [keep.tile([P, N], F32, name="capped%d" % m, align_bytes=64) for m in range(2)]
+        result = [keep.tile([P, N], F32, name="result%d" % m, align_bytes=64) for m in range(2)]
+        stores = {0: 0, 1: 0, 2: 256, 3: 256}
+        for u, (m, s0, w) in enumerate(units):
+            slots = slice(s0, s0 + w)
+            product(u, cw, cs, C_ROW, False)
+            nc.scalar.activation(capped[m][:, slots], acc[u][:], TANH, bias=no_bias[:], scale=1.0 / CAP)
+            if u in stores:
+                done = slice(stores[u], s0 + w)
+                nc.vector.tensor_scalar_mul(result[m][:, done], capped[m][:, done], CAP)
+                nc.sync.dma_start(out[0, m * P : (m + 1) * P, done], result[m][:, done])

@@ -40,20 +40,24 @@ def tile_attend_residcap_topk_kernel(tc, qT, k_words, k_scales, c_words, c_scale
         nc.vector.memset(zero[:], 0.0)
         nc.vector.memset(cs_pool[:], 0)
 
-        def load_scales(engines, pool_tile, scales, first_row):
-            rows = scales[0].bitcast(I32)
-            for r, eng in enumerate(engines):
-                eng.dma_start(pool_tile[first_row + r : P : 32, :], rows[r:16:4, :])
+        def load_scales(pool_tile, scales, first_row):
+            nc.sync.dma_start(pool_tile[first_row:P:8, :], scales[0].bitcast(I32))
+
+        def place_scales(plane, gathered, first_row):
+            rows = gathered[:].bitcast(I32)
+            nc.vector.tensor_copy(plane[:], rows)
+            for r in range(1, 4):
+                nc.scalar.dma_start(plane[first_row + r : P : 32, :], rows[first_row + 8 * r : P : 32, :])
 
         def load_words(pool_tile, words):
             nc.sync.dma_start(pool_tile[:], words[0].rearrange("p n t -> p (n t)").bitcast(I32))
 
         nc.sync.dma_start(q_raw[:], qT[0].rearrange("(p j) w -> p j w", j=PACK))
         nc.sync.dma_start(offsets[:], offs)
-        load_scales([nc.sync, nc.sync, nc.scalar, nc.scalar], ks_pool, k_scales, 0)
+        load_scales(ks_pool, k_scales, 0)
+        load_scales(cs_pool, c_scales, C_ROW)
         nc.scalar.activation(no_bias[:], zero[:], TANH)
         load_words(kw_pool, k_words)
-        load_scales([nc.sync] * 4, cs_pool, c_scales, C_ROW)
         load_words(cw_pool, c_words)
 
         q_grouped = keep.tile([P, NQ, PACK], BF16, name="q_grouped", align_bytes=64)
@@ -64,17 +68,21 @@ def tile_attend_residcap_topk_kernel(tc, qT, k_words, k_scales, c_words, c_scale
         ks = keep.tile([P, N], U8, name="ks", align_bytes=64)
         cs = keep.tile([P, N], U8, name="cs", align_bytes=64)
 
+        k_plane = keep.tile([P, N // 4], I32, name="k_plane", align_bytes=64)
+        c_plane = keep.tile([P, N // 4], I32, name="c_plane", align_bytes=64)
+
         q_by_column = q_raw[:].rearrange("p j w -> p w j")
-        nc.scalar.copy(q_grouped[:, 0:P, :], q_by_column[:, 0:P, :])
-        nc.vector.tensor_copy(q_grouped[:, P:NQ, :], q_by_column[:, P:NQ, :])
+        nc.scalar.copy(q_grouped[:], q_by_column)
         nc.vector.tensor_copy(ks[:], ks_pool[:].bitcast(U8).indirect(offsets[:]))
+        place_scales(k_plane, ks, 0)
+        nc.vector.tensor_copy(cs[:], cs_pool[:].bitcast(U8).indirect(offsets[:]))
+        place_scales(c_plane, cs, C_ROW)
         nc.vector.quantize_mx(
             out=q_codes[:].bitcast(FP8X4),
             scales=q_scales[:],
             in_=q_grouped[:].rearrange("p w j -> p (w j)"),
         )
         nc.vector.tensor_copy(kw[:], kw_pool[:].bitcast(U32).indirect(offsets[:]))
-        nc.vector.tensor_copy(cs[:], cs_pool[:].bitcast(U8).indirect(offsets[:]))
 
         units = [(0, 0, 256), (1, 0, 256), (0, 256, 256), (1, 256, 256)]
         acc = [psum.tile([P, w], F32, name="acc%d" % u) for u, (m, s0, w) in enumerate(units)]
@@ -88,13 +96,13 @@ def tile_attend_residcap_topk_kernel(tc, qT, k_words, k_scales, c_words, c_scale
                 lhsT=q_codes[:, rows].bitcast(FP8X4),
                 lhsT_scale=q_scales[:, rows],
                 rhs=words[:, slots].bitcast(FP8X4),
-                rhs_scale=scales[first_row:P, slots],
+                rhs_scale=scales[:].bitcast(U8)[first_row:P, slots],
                 start=start,
                 stop=not start,
             )
 
         for u in range(len(units)):
-            product(u, kw, ks, 0, True)
+            product(u, kw, k_plane, 0, True)
 
         for h in range(2):
             slots = slice(h * HALF, (h + 1) * HALF)
@@ -105,7 +113,7 @@ def tile_attend_residcap_topk_kernel(tc, qT, k_words, k_scales, c_words, c_scale
         stores = {0: 0, 1: 0, 2: 256, 3: 256}
         for u, (m, s0, w) in enumerate(units):
             slots = slice(s0, s0 + w)
-            product(u, cw, cs, C_ROW, False)
+            product(u, cw, c_plane, C_ROW, False)
             nc.scalar.activation(capped[m][:, slots], acc[u][:], TANH, bias=no_bias[:], scale=1.0 / CAP)
             if u in stores:
                 done = slice(stores[u], s0 + w)

@@ -33,12 +33,13 @@ def tile_attend_residcap_topk_kernel(tc, qT, k_words, k_scales, c_words, c_scale
         cw_pool = keep.tile([P, T], I32, name="cw_pool", align_bytes=64)
         ks_pool = keep.tile([P, T // 4], I32, name="ks_pool", align_bytes=64)
         cs_pool = keep.tile([P, T // 4], I32, name="cs_pool", align_bytes=64)
+        c_plane = keep.tile([P, N // 4], I32, name="c_plane", align_bytes=64)
         zero = keep.tile([P, 1], F32, name="zero")
         no_bias = keep.tile([P, 1], F32, name="no_bias")
 
+        nc.gpsimd.memset(cs_pool[:], 0)
         nc.vector.memset(ks_pool[:], 0)
         nc.vector.memset(zero[:], 0.0)
-        nc.vector.memset(cs_pool[:], 0)
 
         def load_scales(pool_tile, scales, first_row):
             nc.sync.dma_start(pool_tile[first_row:P:8, :], scales[0].bitcast(I32))
@@ -54,35 +55,36 @@ def tile_attend_residcap_topk_kernel(tc, qT, k_words, k_scales, c_words, c_scale
 
         nc.sync.dma_start(q_raw[:], qT[0].rearrange("(p j) w -> p j w", j=PACK))
         nc.sync.dma_start(offsets[:], offs)
-        load_scales(ks_pool, k_scales, 0)
         load_scales(cs_pool, c_scales, C_ROW)
+        for r in range(4):
+            nc.sync.dma_start(ks_pool[r:P:32, :], k_scales[0].bitcast(I32)[r:16:4, :])
         nc.scalar.activation(no_bias[:], zero[:], TANH)
         load_words(kw_pool, k_words)
         load_words(cw_pool, c_words)
 
         q_grouped = keep.tile([P, NQ, PACK], BF16, name="q_grouped", align_bytes=64)
-        q_codes = keep.tile([P, NQ], U32, name="q_codes", align_bytes=64)
         q_scales = keep.tile([P, NQ], U8, name="q_scales", align_bytes=64)
         kw = keep.tile([P, N], U32, name="kw", align_bytes=64)
         cw = keep.tile([P, N], U32, name="cw", align_bytes=64)
         ks = keep.tile([P, N], U8, name="ks", align_bytes=64)
         cs = keep.tile([P, N], U8, name="cs", align_bytes=64)
 
-        k_plane = keep.tile([P, N // 4], I32, name="k_plane", align_bytes=64)
-        c_plane = keep.tile([P, N // 4], I32, name="c_plane", align_bytes=64)
 
         q_by_column = q_raw[:].rearrange("p j w -> p w j")
         nc.scalar.copy(q_grouped[:], q_by_column)
-        nc.vector.tensor_copy(ks[:], ks_pool[:].bitcast(U8).indirect(offsets[:]))
-        place_scales(k_plane, ks, 0)
         nc.vector.tensor_copy(cs[:], cs_pool[:].bitcast(U8).indirect(offsets[:]))
-        place_scales(c_plane, cs, C_ROW)
+        q_codes = keep.tile([P, NQ], U32, name="q_codes", align_bytes=64)
         nc.vector.quantize_mx(
             out=q_codes[:].bitcast(FP8X4),
             scales=q_scales[:],
             in_=q_grouped[:].rearrange("p w j -> p (w j)"),
         )
-        nc.vector.tensor_copy(kw[:], kw_pool[:].bitcast(U32).indirect(offsets[:]))
+        place_scales(c_plane, cs, C_ROW)
+        nc.vector.tensor_copy(ks[:], ks_pool[:].bitcast(U8).indirect(offsets[:]))
+        for h in range(2):
+            slots = slice(h * HALF, (h + 1) * HALF)
+            cols = slice(h * HALF // 16, (h + 1) * HALF // 16)
+            nc.vector.tensor_copy(kw[:, slots], kw_pool[:].bitcast(U32).indirect(offsets[:, cols]))
 
         units = [(0, 0, 256), (1, 0, 256), (0, 256, 256), (1, 256, 256)]
         acc = [psum.tile([P, w], F32, name="acc%d" % u) for u, (m, s0, w) in enumerate(units)]
@@ -96,13 +98,13 @@ def tile_attend_residcap_topk_kernel(tc, qT, k_words, k_scales, c_words, c_scale
                 lhsT=q_codes[:, rows].bitcast(FP8X4),
                 lhsT_scale=q_scales[:, rows],
                 rhs=words[:, slots].bitcast(FP8X4),
-                rhs_scale=scales[:].bitcast(U8)[first_row:P, slots],
+                rhs_scale=scales[first_row:P, slots],
                 start=start,
                 stop=not start,
             )
 
         for u in range(len(units)):
-            product(u, kw, k_plane, 0, True)
+            product(u, kw, ks, 0, True)
 
         for h in range(2):
             slots = slice(h * HALF, (h + 1) * HALF)
@@ -113,7 +115,7 @@ def tile_attend_residcap_topk_kernel(tc, qT, k_words, k_scales, c_words, c_scale
         stores = {0: 0, 1: 0, 2: 256, 3: 256}
         for u, (m, s0, w) in enumerate(units):
             slots = slice(s0, s0 + w)
-            product(u, cw, c_plane, C_ROW, False)
+            product(u, cw, c_plane[:].bitcast(U8), C_ROW, False)
             nc.scalar.activation(capped[m][:, slots], acc[u][:], TANH, bias=no_bias[:], scale=1.0 / CAP)
             if u in stores:
                 done = slice(stores[u], s0 + w)

@@ -37,7 +37,7 @@ def tile_attend_residcap_topk_kernel(tc, qT, k_words, k_scales, c_words, c_scale
         zero = keep.tile([P, 1], F32, name="zero")
         no_bias = keep.tile([P, 1], F32, name="no_bias")
 
-        nc.gpsimd.memset(cs_pool[:], 0)
+        nc.vector.memset(cs_pool[:], 0)
         nc.vector.memset(ks_pool[:], 0)
         nc.vector.memset(zero[:], 0.0)
 

@@ -86,7 +86,7 @@ def tile_attend_residcap_topk_kernel(tc, qT, k_words, k_scales, c_words, c_scale
             cols = slice(h * HALF // 16, (h + 1) * HALF // 16)
             nc.vector.tensor_copy(kw[:, slots], kw_pool[:].bitcast(U32).indirect(offsets[:, cols]))
 
-        units = [(0, 0, 256), (1, 0, 256), (0, 256, 256), (1, 256, 256)]
+        units = [(0, 0, 256), (1, 0, 256), (0, 256, 128), (0, 384, 128), (1, 256, 128), (1, 384, 128)]
         acc = [psum.tile([P, w], F32, name="acc%d" % u) for u, (m, s0, w) in enumerate(units)]
 
         def product(u, words, scales, first_row, start):
@@ -112,12 +112,11 @@ def tile_attend_residcap_topk_kernel(tc, qT, k_words, k_scales, c_words, c_scale
             nc.vector.tensor_copy(cw[:, slots], cw_pool[:].bitcast(U32).indirect(offsets[:, cols]))
         capped = [keep.tile([P, N], F32, name="capped%d" % m, align_bytes=64) for m in range(2)]
         result = [keep.tile([P, N], F32, name="result%d" % m, align_bytes=64) for m in range(2)]
-        stores = {0: 0, 1: 0, 2: 256, 3: 256}
         for u, (m, s0, w) in enumerate(units):
             slots = slice(s0, s0 + w)
             product(u, cw, c_plane[:].bitcast(U8), C_ROW, False)
             nc.scalar.activation(capped[m][:, slots], acc[u][:], TANH, bias=no_bias[:], scale=1.0 / CAP)
-            if u in stores:
-                done = slice(stores[u], s0 + w)
-                nc.vector.tensor_scalar_mul(result[m][:, done], capped[m][:, done], CAP)
+            nc.vector.tensor_scalar_mul(result[m][:, slots], capped[m][:, slots], CAP)
+            if (s0 + w) % HALF == 0:
+                done = slice(s0 + w - HALF, s0 + w)
                 nc.sync.dma_start(out[0, m * P : (m + 1) * P, done], result[m][:, done])

@@ -86,7 +86,7 @@ def tile_attend_residcap_topk_kernel(tc, qT, k_words, k_scales, c_words, c_scale
             cols = slice(h * HALF // 16, (h + 1) * HALF // 16)
             nc.vector.tensor_copy(kw[:, slots], kw_pool[:].bitcast(U32).indirect(offsets[:, cols]))
 
-        units = [(0, 0, 256), (1, 0, 256), (0, 256, 128), (0, 384, 128), (1, 256, 128), (1, 384, 128)]
+        units = [(0, 0, 128), (0, 128, 128), (1, 0, 256), (0, 256, 128), (0, 384, 128), (1, 256, 128), (1, 384, 128)]
         acc = [psum.tile([P, w], F32, name="acc%d" % u) for u, (m, s0, w) in enumerate(units)]
 
         def product(u, words, scales, first_row, start):

@@ -86,7 +86,7 @@ def tile_attend_residcap_topk_kernel(tc, qT, k_words, k_scales, c_words, c_scale
             cols = slice(h * HALF // 16, (h + 1) * HALF // 16)
             nc.vector.tensor_copy(kw[:, slots], kw_pool[:].bitcast(U32).indirect(offsets[:, cols]))
 
-        units = [(0, 0, 128), (0, 128, 128), (1, 0, 256), (0, 256, 128), (0, 384, 128), (1, 256, 128), (1, 384, 128)]
+        units = [(m, s0, P) for h in range(2) for m in range(2) for s0 in range(h * HALF, (h + 1) * HALF, P)]
         acc = [psum.tile([P, w], F32, name="acc%d" % u) for u, (m, s0, w) in enumerate(units)]
 
         def product(u, words, scales, first_row, start):

@@ -28,12 +28,12 @@ def tile_attend_residcap_topk_kernel(tc, qT, k_words, k_scales, c_words, c_scale
         psum = ctx.enter_context(tc.psum_pool(name="psum", bufs=1))
 
         offsets = keep.tile([P, N // 16], U16, name="offsets")
-        q_raw = keep.tile([P, PACK, NQ], F32, name="q_raw", align_bytes=64)
-        kw_pool = keep.tile([P, T], I32, name="kw_pool", align_bytes=64)
-        cw_pool = keep.tile([P, T], I32, name="cw_pool", align_bytes=64)
-        ks_pool = keep.tile([P, T // 4], I32, name="ks_pool", align_bytes=64)
-        cs_pool = keep.tile([P, T // 4], I32, name="cs_pool", align_bytes=64)
-        c_plane = keep.tile([P, N // 4], I32, name="c_plane", align_bytes=64)
+        q_raw = keep.tile([P, PACK, NQ], F32, name="q_raw", align_bytes=256)
+        kw_pool = keep.tile([P, T], I32, name="kw_pool", align_bytes=256)
+        cw_pool = keep.tile([P, T], I32, name="cw_pool", align_bytes=256)
+        ks_pool = keep.tile([P, T // 4], I32, name="ks_pool", align_bytes=256)
+        cs_pool = keep.tile([P, T // 4], I32, name="cs_pool", align_bytes=256)
+        c_plane = keep.tile([P, N // 4], I32, name="c_plane", align_bytes=256)
         zero = keep.tile([P, 1], F32, name="zero")
         no_bias = keep.tile([P, 1], F32, name="no_bias")
 
@@ -62,18 +62,18 @@ def tile_attend_residcap_topk_kernel(tc, qT, k_words, k_scales, c_words, c_scale
         load_words(kw_pool, k_words)
         load_words(cw_pool, c_words)
 
-        q_grouped = keep.tile([P, NQ, PACK], BF16, name="q_grouped", align_bytes=64)
-        q_scales = keep.tile([P, NQ], U8, name="q_scales", align_bytes=64)
-        kw = keep.tile([P, N], U32, name="kw", align_bytes=64)
-        cw = keep.tile([P, N], U32, name="cw", align_bytes=64)
-        ks = keep.tile([P, N], U8, name="ks", align_bytes=64)
-        cs = keep.tile([P, N], U8, name="cs", align_bytes=64)
+        q_grouped = keep.tile([P, NQ, PACK], BF16, name="q_grouped", align_bytes=256)
+        q_scales = keep.tile([P, NQ], U8, name="q_scales", align_bytes=256)
+        kw = keep.tile([P, N], U32, name="kw", align_bytes=256)
+        cw = keep.tile([P, N], U32, name="cw", align_bytes=256)
+        ks = keep.tile([P, N], U8, name="ks", align_bytes=256)
+        cs = keep.tile([P, N], U8, name="cs", align_bytes=256)
 
 
         q_by_column = q_raw[:].rearrange("p j w -> p w j")
         nc.scalar.copy(q_grouped[:], q_by_column)
         nc.vector.tensor_copy(cs[:], cs_pool[:].bitcast(U8).indirect(offsets[:]))
-        q_codes = keep.tile([P, NQ], U32, name="q_codes", align_bytes=64)
+        q_codes = keep.tile([P, NQ], U32, name="q_codes", align_bytes=256)
         nc.vector.quantize_mx(
             out=q_codes[:].bitcast(FP8X4),
             scales=q_scales[:],
@@ -110,8 +110,8 @@ def tile_attend_residcap_topk_kernel(tc, qT, k_words, k_scales, c_words, c_scale
             slots = slice(h * HALF, (h + 1) * HALF)
             cols = slice(h * HALF // 16, (h + 1) * HALF // 16)
             nc.vector.tensor_copy(cw[:, slots], cw_pool[:].bitcast(U32).indirect(offsets[:, cols]))
-        capped = [keep.tile([P, N], F32, name="capped%d" % m, align_bytes=64) for m in range(2)]
-        result = [keep.tile([P, N], F32, name="result%d" % m, align_bytes=64) for m in range(2)]
+        capped = [keep.tile([P, N], F32, name="capped%d" % m, align_bytes=256) for m in range(2)]
+        result = [keep.tile([P, N], F32, name="result%d" % m, align_bytes=256) for m in range(2)]
         for u, (m, s0, w) in enumerate(units):
             slots = slice(s0, s0 + w)
             product(u, cw, c_plane[:].bitcast(U8), C_ROW, False)

@@ -17,6 +17,7 @@ D, NQ, T, N = 512, 256, 2048, 512
 CAP = 20.0
 HALF = N // 2
 C_ROW = 4
+QUARTERS = N // P
 
 FLOPS = 2 * 2 * D * NQ * N
 
@@ -86,37 +87,38 @@ def tile_attend_residcap_topk_kernel(tc, qT, k_words, k_scales, c_words, c_scale
             cols = slice(h * HALF // 16, (h + 1) * HALF // 16)
             nc.vector.tensor_copy(kw[:, slots], kw_pool[:].bitcast(U32).indirect(offsets[:, cols]))
 
-        units = [(m, s0, P) for h in range(2) for m in range(2) for s0 in range(h * HALF, (h + 1) * HALF, P)]
-        acc = [psum.tile([P, w], F32, name="acc%d" % u) for u, (m, s0, w) in enumerate(units)]
+        pieces = [(j, (0, 1)) for j in range(QUARTERS - 1)] + [(QUARTERS - 1, (0,)), (QUARTERS - 1, (1,))]
+        acc = [psum.tile([P, len(tiles), P], F32, name="acc%d" % u) for u, (j, tiles) in enumerate(pieces)]
 
-        def product(u, words, scales, first_row, start):
-            m, s0, w = units[u]
-            slots = slice(s0, s0 + w)
-            rows = slice(m * P, (m + 1) * P)
-            nc.tensor.matmul_mx(
-                out=acc[u][:],
-                lhsT=q_codes[:, rows].bitcast(FP8X4),
-                lhsT_scale=q_scales[:, rows],
-                rhs=words[:, slots].bitcast(FP8X4),
-                rhs_scale=scales[first_row:P, slots],
-                start=start,
-                stop=not start,
-            )
+        def products(u, words, scales, first_row, opens):
+            j, tiles = pieces[u]
+            slots = slice(j * P, (j + 1) * P)
+            for place, m in enumerate(tiles):
+                rows = slice(m * P, (m + 1) * P)
+                nc.tensor.matmul_mx(
+                    out=acc[u][:, place, :],
+                    lhsT=q_codes[:, rows].bitcast(FP8X4),
+                    lhsT_scale=q_scales[:, rows],
+                    rhs=words[:, slots].bitcast(FP8X4),
+                    rhs_scale=scales[first_row:P, slots],
+                    start=opens and place == 0,
+                    stop=not opens and place == len(tiles) - 1,
+                )
 
-        for u in range(len(units)):
-            product(u, kw, ks, 0, True)
+        for u in range(len(pieces)):
+            products(u, kw, ks, 0, True)
 
-        for h in range(2):
-            slots = slice(h * HALF, (h + 1) * HALF)
-            cols = slice(h * HALF // 16, (h + 1) * HALF // 16)
+        for j in range(QUARTERS):
+            slots = slice(j * P, (j + 1) * P)
+            cols = slice(j * P // 16, (j + 1) * P // 16)
             nc.vector.tensor_copy(cw[:, slots], cw_pool[:].bitcast(U32).indirect(offsets[:, cols]))
-        capped = [keep.tile([P, N], F32, name="capped%d" % m, align_bytes=256) for m in range(2)]
-        result = [keep.tile([P, N], F32, name="result%d" % m, align_bytes=256) for m in range(2)]
-        for u, (m, s0, w) in enumerate(units):
-            slots = slice(s0, s0 + w)
-            product(u, cw, c_plane[:].bitcast(U8), C_ROW, False)
-            nc.scalar.activation(capped[m][:, slots], acc[u][:], TANH, bias=no_bias[:], scale=1.0 / CAP)
-            nc.vector.tensor_scalar_mul(result[m][:, slots], capped[m][:, slots], CAP)
-            if (s0 + w) % HALF == 0:
-                done = slice(s0 + w - HALF, s0 + w)
-                nc.sync.dma_start(out[0, m * P : (m + 1) * P, done], result[m][:, done])
+        out_by_tile = out[0].rearrange("(m p) s -> p m s", p=P)
+        capped = [keep.tile([P, 2, P], F32, name="capped%d" % j, align_bytes=256) for j in range(QUARTERS)]
+        result = [keep.tile([P, 2, P], F32, name="result%d" % j, align_bytes=256) for j in range(QUARTERS)]
+        for u, (j, tiles) in enumerate(pieces):
+            products(u, cw, c_plane[:].bitcast(U8), C_ROW, False)
+            places = slice(tiles[0], tiles[-1] + 1)
+            nc.scalar.activation(capped[j][:, places, :], acc[u][:], TANH, bias=no_bias[:], scale=1.0 / CAP)
+            nc.vector.tensor_scalar_mul(result[j][:, places, :], capped[j][:, places, :], CAP)
+            if tiles[-1] == 1:
+                nc.sync.dma_start(out_by_tile[:, :, j * P : (j + 1) * P], result[j][:])

@@ -15,7 +15,6 @@ P = 128
 PACK = 4
 D, NQ, T, N = 512, 256, 2048, 512
 CAP = 20.0
-HALF = N // 2
 C_ROW = 4
 QUARTERS = N // P
 
@@ -82,12 +81,14 @@ def tile_attend_residcap_topk_kernel(tc, qT, k_words, k_scales, c_words, c_scale
         )
         place_scales(c_plane, cs, C_ROW)
         nc.vector.tensor_copy(ks[:], ks_pool[:].bitcast(U8).indirect(offsets[:]))
-        for h in range(2):
-            slots = slice(h * HALF, (h + 1) * HALF)
-            cols = slice(h * HALF // 16, (h + 1) * HALF // 16)
+        for j in range(QUARTERS):
+            slots = slice(j * P, (j + 1) * P)
+            cols = slice(j * P // 16, (j + 1) * P // 16)
             nc.vector.tensor_copy(kw[:, slots], kw_pool[:].bitcast(U32).indirect(offsets[:, cols]))
 
-        pieces = [(j, (0, 1)) for j in range(QUARTERS - 1)] + [(QUARTERS - 1, (0,)), (QUARTERS - 1, (1,))]
+        pieces = []
+        for j in range(QUARTERS):
+            pieces += [(j, (0,)), (j, (1,))] if j in (0, QUARTERS - 1) else [(j, (0, 1))]
         acc = [psum.tile([P, len(tiles), P], F32, name="acc%d" % u) for u, (j, tiles) in enumerate(pieces)]
 
         def products(u, words, scales, first_row, opens):

@@ -17,6 +17,7 @@ D, NQ, T, N = 512, 256, 2048, 512
 CAP = 20.0
 C_ROW = 4
 QUARTERS = N // P
+WARM_ROWS, WARM_PASSES = 32, 6
 
 FLOPS = 2 * 2 * D * NQ * N
 
@@ -81,6 +82,19 @@ def tile_attend_residcap_topk_kernel(tc, qT, k_words, k_scales, c_words, c_scale
         )
         place_scales(c_plane, cs, C_ROW)
         nc.vector.tensor_copy(ks[:], ks_pool[:].bitcast(U8).indirect(offsets[:]))
+        warm_rows = keep.tile([P, WARM_ROWS], U32, name="warm_rows", align_bytes=256)
+        nc.scalar.copy(warm_rows[:], q_codes[:, 0:WARM_ROWS])
+        unused = psum.tile([WARM_ROWS, P], F32, name="unused")
+        for w in range(WARM_PASSES):
+            nc.tensor.matmul_mx(
+                out=unused[:],
+                lhsT=warm_rows[:].bitcast(FP8X4),
+                lhsT_scale=q_scales[:, 0:WARM_ROWS],
+                rhs=q_codes[:, P:NQ].bitcast(FP8X4),
+                rhs_scale=q_scales[:, P:NQ],
+                start=True,
+                stop=True,
+            )
         for j in range(QUARTERS):
             slots = slice(j * P, (j + 1) * P)
             cols = slice(j * P // 16, (j + 1) * P // 16)

from contextlib import ExitStack

import concourse.mybir as mybir

F32 = mybir.dt.float32
BF16 = mybir.dt.bfloat16
I32 = mybir.dt.int32
U32 = mybir.dt.uint32
U16 = mybir.dt.uint16
U8 = mybir.dt.uint8
FP8X4 = mybir.dt.float8_e4m3fn_x4
TANH = mybir.ActivationFunctionType.Tanh

P = 128
PACK = 4
D, NQ, T, N = 512, 256, 2048, 512
CAP = 20.0
C_ROW = 4
QUARTERS = N // P
WARM_ROWS, WARM_PASSES = 32, 6

FLOPS = 2 * 2 * D * NQ * N


def tile_attend_residcap_topk_kernel(tc, qT, k_words, k_scales, c_words, c_scales, offs, out):
    nc = tc.nc
    with ExitStack() as ctx:
        keep = ctx.enter_context(tc.tile_pool(name="keep", bufs=1))
        psum = ctx.enter_context(tc.psum_pool(name="psum", bufs=1))

        offsets = keep.tile([P, N // 16], U16, name="offsets")
        q_raw = keep.tile([P, PACK, NQ], F32, name="q_raw", align_bytes=256)
        kw_pool = keep.tile([P, T], I32, name="kw_pool", align_bytes=256)
        cw_pool = keep.tile([P, T], I32, name="cw_pool", align_bytes=256)
        ks_pool = keep.tile([P, T // 4], I32, name="ks_pool", align_bytes=256)
        cs_pool = keep.tile([P, T // 4], I32, name="cs_pool", align_bytes=256)
        c_plane = keep.tile([P, N // 4], I32, name="c_plane", align_bytes=256)
        zero = keep.tile([P, 1], F32, name="zero")
        no_bias = keep.tile([P, 1], F32, name="no_bias")

        nc.vector.memset(cs_pool[:], 0)
        nc.vector.memset(ks_pool[:], 0)
        nc.vector.memset(zero[:], 0.0)

        def load_scales(pool_tile, scales, first_row):
            nc.sync.dma_start(pool_tile[first_row:P:8, :], scales[0].bitcast(I32))

        def place_scales(plane, gathered, first_row):
            rows = gathered[:].bitcast(I32)
            nc.vector.tensor_copy(plane[:], rows)
            for r in range(1, 4):
                nc.scalar.dma_start(plane[first_row + r : P : 32, :], rows[first_row + 8 * r : P : 32, :])

        def load_words(pool_tile, words):
            nc.sync.dma_start(pool_tile[:], words[0].rearrange("p n t -> p (n t)").bitcast(I32))

        nc.sync.dma_start(q_raw[:], qT[0].rearrange("(p j) w -> p j w", j=PACK))
        nc.sync.dma_start(offsets[:], offs)
        load_scales(cs_pool, c_scales, C_ROW)
        for r in range(4):
            nc.sync.dma_start(ks_pool[r:P:32, :], k_scales[0].bitcast(I32)[r:16:4, :])
        nc.scalar.activation(no_bias[:], zero[:], TANH)
        load_words(kw_pool, k_words)
        load_words(cw_pool, c_words)

        q_grouped = keep.tile([P, NQ, PACK], BF16, name="q_grouped", align_bytes=256)
        q_scales = keep.tile([P, NQ], U8, name="q_scales", align_bytes=256)
        kw = keep.tile([P, N], U32, name="kw", align_bytes=256)
        cw = keep.tile([P, N], U32, name="cw", align_bytes=256)
        ks = keep.tile([P, N], U8, name="ks", align_bytes=256)
        cs = keep.tile([P, N], U8, name="cs", align_bytes=256)


        q_by_column = q_raw[:].rearrange("p j w -> p w j")
        nc.scalar.copy(q_grouped[:], q_by_column)
        nc.vector.tensor_copy(cs[:], cs_pool[:].bitcast(U8).indirect(offsets[:]))
        q_codes = keep.tile([P, NQ], U32, name="q_codes", align_bytes=256)
        nc.vector.quantize_mx(
            out=q_codes[:].bitcast(FP8X4),
            scales=q_scales[:],
            in_=q_grouped[:].rearrange("p w j -> p (w j)"),
        )
        place_scales(c_plane, cs, C_ROW)
        nc.vector.tensor_copy(ks[:], ks_pool[:].bitcast(U8).indirect(offsets[:]))
        warm_rows = keep.tile([P, WARM_ROWS], U32, name="warm_rows", align_bytes=256)
        nc.scalar.copy(warm_rows[:], q_codes[:, 0:WARM_ROWS])
        unused = psum.tile([WARM_ROWS, P], F32, name="unused")
        for w in range(WARM_PASSES):
            nc.tensor.matmul_mx(
                out=unused[:],
                lhsT=warm_rows[:].bitcast(FP8X4),
                lhsT_scale=q_scales[:, 0:WARM_ROWS],
                rhs=q_codes[:, P:NQ].bitcast(FP8X4),
                rhs_scale=q_scales[:, P:NQ],
                start=True,
                stop=True,
            )
        for j in range(QUARTERS):
            slots = slice(j * P, (j + 1) * P)
            cols = slice(j * P // 16, (j + 1) * P // 16)
            nc.vector.tensor_copy(kw[:, slots], kw_pool[:].bitcast(U32).indirect(offsets[:, cols]))

        pieces = []
        for j in range(QUARTERS):
            pieces += [(j, (0,)), (j, (1,))] if j in (0, QUARTERS - 1) else [(j, (0, 1))]
        acc = [psum.tile([P, len(tiles), P], F32, name="acc%d" % u) for u, (j, tiles) in enumerate(pieces)]

        def products(u, words, scales, first_row, opens):
            j, tiles = pieces[u]
            slots = slice(j * P, (j + 1) * P)
            for place, m in enumerate(tiles):
                rows = slice(m * P, (m + 1) * P)
                nc.tensor.matmul_mx(
                    out=acc[u][:, place, :],
                    lhsT=q_codes[:, rows].bitcast(FP8X4),
                    lhsT_scale=q_scales[:, rows],
                    rhs=words[:, slots].bitcast(FP8X4),
                    rhs_scale=scales[first_row:P, slots],
                    start=opens and place == 0,
                    stop=not opens and place == len(tiles) - 1,
                )

        for u in range(len(pieces)):
            products(u, kw, ks, 0, True)

        for j in range(QUARTERS):
            slots = slice(j * P, (j + 1) * P)
            cols = slice(j * P // 16, (j + 1) * P // 16)
            nc.vector.tensor_copy(cw[:, slots], cw_pool[:].bitcast(U32).indirect(offsets[:, cols]))
        out_by_tile = out[0].rearrange("(m p) s -> p m s", p=P)
        capped = [keep.tile([P, 2, P], F32, name="capped%d" % j, align_bytes=256) for j in range(QUARTERS)]
        result = [keep.tile([P, 2, P], F32, name="result%d" % j, align_bytes=256) for j in range(QUARTERS)]
        for u, (j, tiles) in enumerate(pieces):
            products(u, cw, c_plane[:].bitcast(U8), C_ROW, False)
            places = slice(tiles[0], tiles[-1] + 1)
            nc.scalar.activation(capped[j][:, places, :], acc[u][:], TANH, bias=no_bias[:], scale=1.0 / CAP)
            nc.vector.tensor_scalar_mul(result[j][:, places, :], capped[j][:, places, :], CAP)
            if tiles[-1] == 1:
                nc.sync.dma_start(out_by_tile[:, :, j * P : (j + 1) * P], result[j][:])
